import numpy as np
import ml_dtypes


def mxq(x, axis, fmt="e4m3"):
    dtype, down = {"e4m3": (ml_dtypes.float8_e4m3fn, 7), "e5m2": (ml_dtypes.float8_e5m2, 14)}[fmt]
    v = np.moveaxis(np.asarray(x, np.float32).astype(ml_dtypes.bfloat16).astype(np.float64), axis, -1)
    blocks = v.reshape(v.shape[:-1] + (-1, 32))
    amax = np.abs(blocks).max(-1, keepdims=True)
    byte = np.maximum(np.where(amax > 0, np.frexp(amax)[1] - 1 + 127, 0) - down, 1)
    scale = np.exp2(byte - 127.0)
    codes = (blocks / scale).astype(np.float32).astype(dtype).astype(np.float64)
    return np.moveaxis((codes * scale).reshape(v.shape), -1, axis)


WIDE = False


def mx_kscale(k):
    if not WIDE:
        return np.ones(k)
    levels = np.array([10, -10, 5, -5, 0])
    if k % 512:
        return np.exp2(np.random.permutation(np.resize(levels, k // 32))).repeat(32)
    a = np.empty((k // 512, 16))
    for p in range(k // 512):
        a[p, :8] = np.random.permutation(np.resize(levels, 8))
        for g in range(8):
            far = levels[np.abs(levels - a[p, g]) >= 10]
            a[p, g + 8] = far[np.random.randint(len(far))]
    return np.exp2(a.ravel()).repeat(32)


def f64(x):
    return np.asarray(x).astype(np.float64)


def striped(idx):
    return np.tile(idx.reshape(-1, 16).T, (8, 1)).astype(np.uint16)


def unstriped(offs):
    return offs[:16].T.reshape(-1).astype(np.int64)


def striped8(idx):
    return np.concatenate([x.reshape(-1, 16).T for x in idx]).astype(np.uint16)


def runs(offs, k):
    lists = np.stack([offs[16 * r : 16 * r + 16].T.reshape(-1) for r in range(8)]).astype(np.int64)
    return lists[np.arange(k) % 512 // 64]


def pack_weight(w):
    k, n = w.shape
    w = f64(np.asarray(w, np.float32).astype(ml_dtypes.bfloat16)).reshape(k // 32, 32, n)
    amax = np.abs(w).max(1)
    byte = np.clip(np.where(amax > 0, np.frexp(amax)[1] - 1 + 127 - 7, 1), 1, 254)
    scaled = (w * np.exp2(127.0 - byte)[:, None, :]).reshape(k, n).astype(np.float32)
    words = np.ascontiguousarray(scaled.reshape(k // 512, 128, 4, n).transpose(0, 1, 3, 2)).astype(ml_dtypes.float8_e4m3fn).view(np.uint8)
    return words, np.ascontiguousarray(byte.astype(np.uint8).reshape(k // 512, 16, n))


def unpack_weight(words, scales):
    g, p, n, _ = words.shape
    vals = np.ascontiguousarray(words).view(ml_dtypes.float8_e4m3fn).astype(np.float64) * np.repeat(np.exp2(scales.astype(np.float64) - 127.0), 8, axis=1)[..., None]
    return vals.transpose(0, 1, 3, 2).reshape(g * 512, n)

def planes(y):
    n, m = y.shape
    v = y.astype(np.float32).astype(ml_dtypes.bfloat16).astype(np.float64).reshape(n // 32, 32, m)
    top = np.abs(v).max(1)
    byte = np.clip(np.where(top > 0, np.frexp(top)[1] - 1 + 127 - 7, 1), 1, 254)
    codes = (v * np.exp2(127.0 - byte)[:, None, :]).reshape(n, m).astype(np.float32).astype(ml_dtypes.float8_e4m3fn).view(np.uint8)
    words = codes.reshape(n // 512, 128, 4, m).transpose(0, 1, 3, 2)
    return np.ascontiguousarray(words), np.ascontiguousarray(byte.astype(np.uint8).reshape(n // 512, 16, m))


K, T, S, G, H, C, W = 512, 1024, 256, 2048, 512, 512, 128


def setup_inputs():
    n = np.random.standard_normal
    s = mx_kscale(K)[:, None]
    packed_xT = pack_weight(n((K, T)) * s)
    packed_dT = pack_weight(n((K, G)) / s)
    perm = np.random.permutation(S)
    return {
        "x_words": packed_xT[0],
        "x_scales": packed_xT[1],
        "d_words": packed_dT[0],
        "d_scales": packed_dT[1],
        "gs": (np.random.uniform(0.5, 1.5, (K, 1)) / s).astype(np.float32),
        "offs": striped(np.random.permutation(T)[:S]),
        "ka": striped8(np.random.randint(0, G, (8, H))),
        "kb": striped8(np.random.randint(0, G, (8, H))),
        "cand": striped(np.random.permutation(T)[:C]),
        "n1": striped(perm[:W]),
        "n2": striped(perm[W:]),
    }


def reference(x_words, x_scales, d_words, d_scales, gs, offs, ka, kb, cand, n1, n2):
    x_cand = unpack_weight(x_words, x_scales)[:, unstriped(cand)]
    d_ka = unpack_weight(d_words, d_scales)[np.arange(K)[:, None], runs(ka, K)]
    xq = unpack_weight(x_words, x_scales)[:, unstriped(offs)]
    d_kb = unpack_weight(d_words, d_scales)[np.arange(K)[:, None], runs(kb, K)]
    h = 0.0625 * (d_ka.T @ xq + d_kb.T @ xq)
    z = f64(gs) * h
    s = 0.0625 * ((x_cand.T @ mxq(z, 0, "e4m3")))
    pa = s[:, unstriped(n1)]
    pb = s[:, unstriped(n2)]
    ra = np.maximum(pa, pb)
    out = s.copy()
    out[:, unstriped(n1)] = ra
    return (out,) + planes(out)

@@ -1,0 +1,154 @@
+from contextlib import ExitStack
+
+import concourse.mybir as mybir
+from concourse.masks import make_identity
+
+F32 = mybir.dt.float32
+BF16 = mybir.dt.bfloat16
+I32 = mybir.dt.int32
+U32 = mybir.dt.uint32
+U16 = mybir.dt.uint16
+U8 = mybir.dt.uint8
+FP8X4 = mybir.dt.float8_e4m3fn_x4
+COPY = mybir.ActivationFunctionType.Copy
+MULT = mybir.AluOpType.mult
+MAX = mybir.AluOpType.max
+
+P = 128
+PACK = 4
+K, T, S, G, H, C, W = 512, 1024, 256, 2048, 512, 512, 128
+SIXTEENTH = 0.0625
+FLOPS = 2 * K * H * S * 2 + 2 * H * C * S
+
+
+def tile_picked_aqcifill_none_po_kernel(tc, x_words, x_scales, d_words, d_scales, gs, offs, ka, kb, cand, n1, n2, out_0, out_1, out_2):
+    nc = tc.nc
+    with ExitStack() as ctx:
+        keep = ctx.enter_context(tc.tile_pool(name="keep", bufs=1))
+        psum = ctx.enter_context(tc.psum_pool(name="psum", bufs=1))
+
+        def load_list(name, source):
+            tile = keep.tile(list(source.shape), U16, name=name)
+            nc.sync.dma_start(tile[:], source)
+            return tile
+
+        d_scale_table = keep.tile([P, G], U8, name="d_scale_table", align_bytes=64)
+        x_scale_table = keep.tile([P, T], U8, name="x_scale_table", align_bytes=64)
+        first_plane = keep.tile([P, 2 * H + S], U8, name="first_plane", align_bytes=64)
+        xc_plane = keep.tile([P, C], U8, name="xc_plane", align_bytes=64)
+        nc.vector.memset(first_plane[:].bitcast(I32), 0)
+        nc.vector.memset(xc_plane[:].bitcast(I32), 0)
+
+        def place_scale_rows(plane, picked):
+            for a in range(4):
+                nc.sync.dma_start(plane[a:P:32, :].bitcast(I32), picked[8 * a : P : 32, :].bitcast(I32))
+
+        ka_list = load_list("ka_list", ka)
+        nc.sync.dma_start(d_scale_table[:].bitcast(I32), d_scales[0].bitcast(I32).unsqueeze(1).to_broadcast([16, 8, G // 4]))
+        kb_list = load_list("kb_list", kb)
+        nc.sync.dma_start(x_scale_table[:].bitcast(I32), x_scales[0].bitcast(I32).unsqueeze(1).to_broadcast([16, 8, T // 4]))
+        offs_list = load_list("offs_list", offs)
+        x_table = keep.tile([P, T], U32, name="x_table", align_bytes=64)
+        nc.sync.dma_start(x_table[:].bitcast(I32), x_words[0].rearrange("p c r -> p (c r)").bitcast(I32))
+        d_table = keep.tile([P, G], U32, name="d_table", tag="d_table", align_bytes=64)
+        nc.sync.dma_start(d_table[:].bitcast(I32), d_words[0].rearrange("p c r -> p (c r)").bitcast(I32))
+        cand_list = load_list("cand_list", cand)
+        n1_list = load_list("n1_list", n1)
+        n2_list = load_list("n2_list", n2)
+
+        gs_col = keep.tile([P, PACK], F32, name="gs_col")
+        nc.gpsimd.dma_start(gs_col[:], gs.rearrange("(p t) o -> p (t o)", t=PACK))
+        ident = keep.tile([P, P], F32, name="ident")
+        make_identity(nc, ident[:])
+
+        first_picked = keep.tile([P, 2 * H + S], U8, name="first_picked", align_bytes=64)
+        nc.vector.tensor_copy(first_picked[:, 0:H], d_scale_table[:].indirect(ka_list[:]))
+        nc.vector.tensor_copy(first_picked[:, H : 2 * H], d_scale_table[:].indirect(kb_list[:]))
+        nc.vector.tensor_copy(first_picked[:, 2 * H : 2 * H + S], x_scale_table[:].indirect(offs_list[:]))
+        place_scale_rows(first_plane, first_picked)
+        xq_words = keep.tile([P, S], U32, name="xq_words", align_bytes=64)
+        nc.vector.tensor_copy(xq_words[:], x_table[:].indirect(offs_list[:]))
+        da_words = keep.tile([P, H], U32, name="da_words", align_bytes=64)
+        db_words = keep.tile([P, H], U32, name="db_words", align_bytes=64)
+        nc.vector.tensor_copy(da_words[:], d_table[:].indirect(ka_list[:]))
+        nc.vector.tensor_copy(db_words[:], d_table[:].indirect(kb_list[:]))
+
+        gs_bank = psum.tile([P, PACK, P], F32, name="gs_bank", tag="shared")
+        for t in range(PACK):
+            nc.tensor.transpose(gs_bank[:, t, :], gs_col[:, t : t + 1].to_broadcast([P, P]), ident[:])
+        gs_row = keep.tile([P, H], F32, name="gs_row", tag="gs_row", align_bytes=64)
+        nc.scalar.activation(gs_row[:].rearrange("q (p t) -> q p t", t=PACK), gs_bank[:].rearrange("q t p -> q p t"), COPY, scale=SIXTEENTH)
+
+        h_banks = [psum.tile([P, H], F32, name="h_bank%d" % b) for b in range(2)]
+        for part, words in enumerate((da_words, db_words)):
+            for b in range(2):
+                nc.tensor.matmul_mx(
+                    out=h_banks[b][:],
+                    lhsT=xq_words[:, b * P : (b + 1) * P].bitcast(FP8X4),
+                    lhsT_scale=first_plane[:, 2 * H + b * P : 2 * H + (b + 1) * P],
+                    rhs=words[:].bitcast(FP8X4),
+                    rhs_scale=first_plane[:, part * H : (part + 1) * H],
+                    start=(part == 0),
+                    stop=(part == 1),
+                )
+
+        xc_picked = keep.tile([P, C], U8, name="xc_picked", tag="d_table", align_bytes=64)
+        nc.vector.tensor_copy(xc_picked[:].rearrange("p (t m) -> p m t", t=PACK), x_scale_table[:].indirect(cand_list[:]))
+        place_scale_rows(xc_plane, xc_picked)
+
+        z_grouped = keep.tile([P, S * PACK], BF16, name="z_grouped", align_bytes=64)
+        z_words = keep.tile([P, S], U32, name="z_words", align_bytes=64)
+        z_plane = keep.tile([P, S], U8, name="z_plane", align_bytes=64)
+        for b in range(2):
+            z_rows = keep.tile([P, H], BF16, name="z_rows%d" % b, align_bytes=64)
+            nc.vector.tensor_tensor(z_rows[:], h_banks[b][:], gs_row[:], MULT)
+            pairs = z_rows[:].bitcast(F32)
+            turn = psum.tile([P, 2, P], F32, name="turn%d" % b)
+            for u in range(2):
+                nc.tensor.transpose(turn[:, u, :], pairs[:, u : H // 2 : 2], ident[:])
+            nc.scalar.copy(
+                z_grouped[:, b * H : (b + 1) * H].bitcast(F32).rearrange("p (r u) -> p r u", u=2),
+                turn[:].rearrange("p u r -> p r u"),
+            )
+
+        xc_words = keep.tile([P, C], U32, name="xc_words", tag="gs_row", align_bytes=64)
+        nc.vector.tensor_copy(xc_words[:].rearrange("p (t m) -> p m t", t=PACK), x_table[:].indirect(cand_list[:]))
+
+        for b in range(2):
+            nc.vector.quantize_mx(
+                out=z_words[:, b * P : (b + 1) * P].bitcast(FP8X4),
+                scales=z_plane[:, b * P : (b + 1) * P],
+                in_=z_grouped[:, b * H : (b + 1) * H],
+            )
+
+        out_rows = out_0.rearrange("(p t) j -> p t j", t=PACK)
+        y_grouped = keep.tile([P, S, PACK], BF16, name="y_grouped", align_bytes=64)
+        for t in range(PACK):
+            s_bank = psum.tile([P, S], F32, name="s_bank%d" % t, tag="shared" if t == 3 else "s_bank%d" % t)
+            nc.tensor.matmul_mx(
+                out=s_bank[:],
+                lhsT=xc_words[:, t * P : (t + 1) * P].bitcast(FP8X4),
+                lhsT_scale=xc_plane[:, t * P : (t + 1) * P],
+                rhs=z_words[:].bitcast(FP8X4),
+                rhs_scale=z_plane[:],
+                start=True,
+                stop=True,
+            )
+            s_tile = keep.tile([P, S], F32, name="s_tile%d" % t, align_bytes=64)
+            nc.vector.tensor_scalar(s_tile[:], s_bank[:], SIXTEENTH, None, MULT)
+            pair = keep.tile([P, 2 * W], F32, name="pair%d" % t, align_bytes=64)
+            nc.scalar.activation(pair[:, 0:W], s_tile[:].indirect(n1_list[:]), COPY)
+            nc.scalar.activation(pair[:, W : 2 * W], s_tile[:].indirect(n2_list[:]), COPY)
+            larger = keep.tile([P, W], F32, name="larger%d" % t, align_bytes=64)
+            nc.vector.tensor_tensor(larger[:], pair[:, 0:W], pair[:, W : 2 * W], MAX)
+            nc.scalar.activation(s_tile[:].indirect(n1_list[:]), larger[:], COPY)
+            nc.sync.dma_start(out_rows[:, t, :], s_tile[:])
+            nc.vector.tensor_copy(y_grouped[:, :, t], s_tile[:])
+
+        y_words = keep.tile([P, S], U32, name="y_words", align_bytes=64)
+        y_plane = keep.tile([P, S], U8, name="y_plane", align_bytes=64)
+        nc.vector.quantize_mx(out=y_words[:].bitcast(FP8X4), scales=y_plane[:], in_=y_grouped[:].rearrange("p j t -> p (j t)"))
+        nc.sync.dma_start(out_1[0].rearrange("p c r -> p (c r)").bitcast(I32), y_words[:].bitcast(I32))
+        for q in range(4):
+            queue = nc.scalar if q % 2 == 0 else nc.sync
+            queue.dma_start(out_2[0, 4 * q : 4 * q + 4, :].bitcast(I32), y_plane[32 * q : 32 * q + 4, :].bitcast(I32))

@@ -34,25 +34,25 @@ def tile_picked_aqcifill_none_po_kernel(tc, x_words, x_scales, d_words, d_scales
 
         d_scale_table = keep.tile([P, G], U8, name="d_scale_table", align_bytes=64)
         x_scale_table = keep.tile([P, T], U8, name="x_scale_table", align_bytes=64)
-        first_plane = keep.tile([P, 2 * H + S], U8, name="first_plane", align_bytes=64)
+        planes = keep.tile([P, 2 * H + S], U8, name="planes", align_bytes=64)
         xc_plane = keep.tile([P, C], U8, name="xc_plane", align_bytes=64)
-        nc.vector.memset(first_plane[:].bitcast(I32), 0)
+        nc.vector.memset(planes[:].bitcast(I32), 0)
         nc.vector.memset(xc_plane[:].bitcast(I32), 0)
 
-        def place_scale_rows(plane, picked):
+        def place_scale_rows(plane, source, queues):
             for a in range(4):
-                nc.sync.dma_start(plane[a:P:32, :].bitcast(I32), picked[8 * a : P : 32, :].bitcast(I32))
+                queues[a % len(queues)].dma_start(plane[a:P:32, :].bitcast(I32), source[8 * a : P : 32, :].bitcast(I32))
 
-        ka_list = load_list("ka_list", ka)
-        nc.sync.dma_start(d_scale_table[:].bitcast(I32), d_scales[0].bitcast(I32).unsqueeze(1).to_broadcast([16, 8, G // 4]))
-        kb_list = load_list("kb_list", kb)
-        nc.sync.dma_start(x_scale_table[:].bitcast(I32), x_scales[0].bitcast(I32).unsqueeze(1).to_broadcast([16, 8, T // 4]))
         offs_list = load_list("offs_list", offs)
+        nc.scalar.dma_start(x_scale_table[:].bitcast(I32), x_scales[0].bitcast(I32).unsqueeze(1).to_broadcast([16, 8, T // 4]))
+        ka_list = load_list("ka_list", ka)
+        nc.scalar.dma_start(d_scale_table[:].bitcast(I32), d_scales[0].bitcast(I32).unsqueeze(1).to_broadcast([16, 8, G // 4]))
+        kb_list = load_list("kb_list", kb)
         x_table = keep.tile([P, T], U32, name="x_table", align_bytes=64)
         nc.sync.dma_start(x_table[:].bitcast(I32), x_words[0].rearrange("p c r -> p (c r)").bitcast(I32))
-        d_table = keep.tile([P, G], U32, name="d_table", tag="d_table", align_bytes=64)
-        nc.sync.dma_start(d_table[:].bitcast(I32), d_words[0].rearrange("p c r -> p (c r)").bitcast(I32))
         cand_list = load_list("cand_list", cand)
+        d_table = keep.tile([P, G], U32, name="d_table", align_bytes=64)
+        nc.sync.dma_start(d_table[:].bitcast(I32), d_words[0].rearrange("p c r -> p (c r)").bitcast(I32))
         n1_list = load_list("n1_list", n1)
         n2_list = load_list("n2_list", n2)
 
@@ -61,49 +61,59 @@ def tile_picked_aqcifill_none_po_kernel(tc, x_words, x_scales, d_words, d_scales
         ident = keep.tile([P, P], F32, name="ident")
         make_identity(nc, ident[:])
 
-        first_picked = keep.tile([P, 2 * H + S], U8, name="first_picked", align_bytes=64)
-        nc.vector.tensor_copy(first_picked[:, 0:H], d_scale_table[:].indirect(ka_list[:]))
-        nc.vector.tensor_copy(first_picked[:, H : 2 * H], d_scale_table[:].indirect(kb_list[:]))
-        nc.vector.tensor_copy(first_picked[:, 2 * H : 2 * H + S], x_scale_table[:].indirect(offs_list[:]))
-        place_scale_rows(first_plane, first_picked)
+        XQ, DA, DB = 0, S, S + H
+        picked = keep.tile([P, 2 * H + S], U8, name="picked", align_bytes=64)
+        nc.vector.tensor_copy(picked[:, XQ : XQ + S], x_scale_table[:].indirect(offs_list[:]))
+        nc.vector.tensor_copy(picked[:, DA : DA + H], d_scale_table[:].indirect(ka_list[:]))
+        nc.vector.tensor_copy(picked[:, DB : DB + H], d_scale_table[:].indirect(kb_list[:]))
+        place_scale_rows(planes, picked, (nc.sync, nc.scalar))
+        xc_picked = keep.tile([P, C], U8, name="xc_picked", align_bytes=64)
+        nc.vector.tensor_copy(xc_picked[:].rearrange("p (t m) -> p m t", t=PACK), x_scale_table[:].indirect(cand_list[:]))
+        place_scale_rows(xc_plane, xc_picked, (nc.sync,))
         xq_words = keep.tile([P, S], U32, name="xq_words", align_bytes=64)
         nc.vector.tensor_copy(xq_words[:], x_table[:].indirect(offs_list[:]))
-        da_words = keep.tile([P, H], U32, name="da_words", align_bytes=64)
-        db_words = keep.tile([P, H], U32, name="db_words", align_bytes=64)
-        nc.vector.tensor_copy(da_words[:], d_table[:].indirect(ka_list[:]))
-        nc.vector.tensor_copy(db_words[:], d_table[:].indirect(kb_list[:]))
+        HALF = H // 2
+        d_picked = {}
+        for f in range(2):
+            for part, codes in enumerate((ka_list, kb_list)):
+                words = keep.tile([P, HALF], U32, name="d_picked%d%d" % (f, part), align_bytes=64)
+                nc.vector.tensor_copy(words[:], d_table[:].indirect(codes[:, f * HALF // 16 : (f + 1) * HALF // 16]))
+                d_picked[f, part] = words
 
-        gs_bank = psum.tile([P, PACK, P], F32, name="gs_bank", tag="shared")
+        gs_bank = psum.tile([P, PACK, P], F32, name="gs_bank", tag="turn0")
         for t in range(PACK):
             nc.tensor.transpose(gs_bank[:, t, :], gs_col[:, t : t + 1].to_broadcast([P, P]), ident[:])
         gs_row = keep.tile([P, H], F32, name="gs_row", tag="gs_row", align_bytes=64)
         nc.scalar.activation(gs_row[:].rearrange("q (p t) -> q p t", t=PACK), gs_bank[:].rearrange("q t p -> q p t"), COPY, scale=SIXTEENTH)
 
-        h_banks = [psum.tile([P, H], F32, name="h_bank%d" % b) for b in range(2)]
-        for part, words in enumerate((da_words, db_words)):
+        h_banks = {}
+        for f in range(2):
             for b in range(2):
-                nc.tensor.matmul_mx(
-                    out=h_banks[b][:],
-                    lhsT=xq_words[:, b * P : (b + 1) * P].bitcast(FP8X4),
-                    lhsT_scale=first_plane[:, 2 * H + b * P : 2 * H + (b + 1) * P],
-                    rhs=words[:].bitcast(FP8X4),
-                    rhs_scale=first_plane[:, part * H : (part + 1) * H],
-                    start=(part == 0),
-                    stop=(part == 1),
-                )
+                h_banks[f, b] = psum.tile([P, HALF], F32, name="h_bank%d%d" % (f, b), tag="bank%d" % (2 * f + b))
+            for part, start in enumerate((DA, DB)):
+                for b in range(2):
+                    nc.tensor.matmul_mx(
+                        out=h_banks[f, b][:],
+                        lhsT=xq_words[:, b * P : (b + 1) * P].bitcast(FP8X4),
+                        lhsT_scale=planes[:, XQ + b * P : XQ + (b + 1) * P],
+                        rhs=d_picked[f, part][:].bitcast(FP8X4),
+                        rhs_scale=planes[:, start + f * HALF : start + (f + 1) * HALF],
+                        start=(part == 0),
+                        stop=(part == 1),
+                    )
 
-        xc_picked = keep.tile([P, C], U8, name="xc_picked", tag="d_table", align_bytes=64)
-        nc.vector.tensor_copy(xc_picked[:].rearrange("p (t m) -> p m t", t=PACK), x_scale_table[:].indirect(cand_list[:]))
-        place_scale_rows(xc_plane, xc_picked)
+        z_rows = [keep.tile([P, H], BF16, name="z_rows%d" % b, align_bytes=64) for b in range(2)]
+        for f in range(2):
+            for b in range(2):
+                cols = slice(f * HALF, (f + 1) * HALF)
+                nc.vector.tensor_tensor(z_rows[b][:, cols], h_banks[f, b][:], gs_row[:, cols], MULT)
 
         z_grouped = keep.tile([P, S * PACK], BF16, name="z_grouped", align_bytes=64)
         z_words = keep.tile([P, S], U32, name="z_words", align_bytes=64)
         z_plane = keep.tile([P, S], U8, name="z_plane", align_bytes=64)
         for b in range(2):
-            z_rows = keep.tile([P, H], BF16, name="z_rows%d" % b, align_bytes=64)
-            nc.vector.tensor_tensor(z_rows[:], h_banks[b][:], gs_row[:], MULT)
-            pairs = z_rows[:].bitcast(F32)
-            turn = psum.tile([P, 2, P], F32, name="turn%d" % b)
+            pairs = z_rows[b][:].bitcast(F32)
+            turn = psum.tile([P, 2, P], F32, name="turn%d" % b, tag="turn%d" % b)
             for u in range(2):
                 nc.tensor.transpose(turn[:, u, :], pairs[:, u : H // 2 : 2], ident[:])
             nc.scalar.copy(
@@ -123,8 +133,9 @@ def tile_picked_aqcifill_none_po_kernel(tc, x_words, x_scales, d_words, d_scales
 
         out_rows = out_0.rearrange("(p t) j -> p t j", t=PACK)
         y_grouped = keep.tile([P, S, PACK], BF16, name="y_grouped", align_bytes=64)
+        s_tiles, pairs_of, larger = [], [], []
         for t in range(PACK):
-            s_bank = psum.tile([P, S], F32, name="s_bank%d" % t, tag="shared" if t == 3 else "s_bank%d" % t)
+            s_bank = psum.tile([P, S], F32, name="s_bank%d" % t, tag="bank%d" % t)
             nc.tensor.matmul_mx(
                 out=s_bank[:],
                 lhsT=xc_words[:, t * P : (t + 1) * P].bitcast(FP8X4),
@@ -139,15 +150,26 @@ def tile_picked_aqcifill_none_po_kernel(tc, x_words, x_scales, d_words, d_scales
             pair = keep.tile([P, 2 * W], F32, name="pair%d" % t, align_bytes=64)
             nc.scalar.activation(pair[:, 0:W], s_tile[:].indirect(n1_list[:]), COPY)
             nc.scalar.activation(pair[:, W : 2 * W], s_tile[:].indirect(n2_list[:]), COPY)
-            larger = keep.tile([P, W], F32, name="larger%d" % t, align_bytes=64)
-            nc.vector.tensor_tensor(larger[:], pair[:, 0:W], pair[:, W : 2 * W], MAX)
-            nc.scalar.activation(s_tile[:].indirect(n1_list[:]), larger[:], COPY)
-            nc.sync.dma_start(out_rows[:, t, :], s_tile[:])
-            nc.vector.tensor_copy(y_grouped[:, :, t], s_tile[:])
+            s_tiles.append(s_tile)
+            pairs_of.append(pair)
+        for t in range(PACK):
+            top = keep.tile([P, W], F32, name="larger%d" % t, align_bytes=64)
+            nc.vector.tensor_tensor(top[:], pairs_of[t][:, 0:W], pairs_of[t][:, W : 2 * W], MAX)
+            larger.append(top)
+        for t in range(PACK):
+            nc.scalar.activation(s_tiles[t][:].indirect(n1_list[:]), larger[t][:], COPY)
+            nc.sync.dma_start(out_rows[:, t, :], s_tiles[t][:])
+            for b in range(2):
+                nc.vector.tensor_copy(y_grouped[:, b * P : (b + 1) * P, t], s_tiles[t][:, b * P : (b + 1) * P])
 
         y_words = keep.tile([P, S], U32, name="y_words", align_bytes=64)
         y_plane = keep.tile([P, S], U8, name="y_plane", align_bytes=64)
-        nc.vector.quantize_mx(out=y_words[:].bitcast(FP8X4), scales=y_plane[:], in_=y_grouped[:].rearrange("p j t -> p (j t)"))
+        for b in range(2):
+            nc.vector.quantize_mx(
+                out=y_words[:, b * P : (b + 1) * P].bitcast(FP8X4),
+                scales=y_plane[:, b * P : (b + 1) * P],
+                in_=y_grouped[:, b * P : (b + 1) * P, :].rearrange("p j t -> p (j t)"),
+            )
         nc.sync.dma_start(out_1[0].rearrange("p c r -> p (c r)").bitcast(I32), y_words[:].bitcast(I32))
         for q in range(4):
             queue = nc.scalar if q % 2 == 0 else nc.sync

@@ -34,6 +34,10 @@ def tile_picked_aqcifill_none_po_kernel(tc, x_words, x_scales, d_words, d_scales
 
         d_scale_table = keep.tile([P, G], U8, name="d_scale_table", align_bytes=64)
         x_scale_table = keep.tile([P, T], U8, name="x_scale_table", align_bytes=64)
+        nc.gpsimd.memset(x_scale_table[:].bitcast(I32), 0)
+        nc.vector.memset(d_scale_table[:].bitcast(I32), 0)
+        ident = keep.tile([P, P], F32, name="ident")
+        make_identity(nc, ident[:])
         planes = keep.tile([P, 2 * H + S], U8, name="planes", align_bytes=64)
         xc_plane = keep.tile([P, C], U8, name="xc_plane", align_bytes=64)
         nc.vector.memset(planes[:].bitcast(I32), 0)
@@ -44,22 +48,20 @@ def tile_picked_aqcifill_none_po_kernel(tc, x_words, x_scales, d_words, d_scales
                 queues[a % len(queues)].dma_start(plane[a:P:32, :].bitcast(I32), source[8 * a : P : 32, :].bitcast(I32))
 
         offs_list = load_list("offs_list", offs)
-        nc.scalar.dma_start(x_scale_table[:].bitcast(I32), x_scales[0].bitcast(I32).unsqueeze(1).to_broadcast([16, 8, T // 4]))
+        nc.scalar.dma_start(x_scale_table[0:P:8, :].bitcast(I32), x_scales[0].bitcast(I32))
         ka_list = load_list("ka_list", ka)
-        nc.scalar.dma_start(d_scale_table[:].bitcast(I32), d_scales[0].bitcast(I32).unsqueeze(1).to_broadcast([16, 8, G // 4]))
+        nc.scalar.dma_start(d_scale_table[0:P:8, :].bitcast(I32), d_scales[0].bitcast(I32))
         kb_list = load_list("kb_list", kb)
-        x_table = keep.tile([P, T], U32, name="x_table", align_bytes=64)
-        nc.sync.dma_start(x_table[:].bitcast(I32), x_words[0].rearrange("p c r -> p (c r)").bitcast(I32))
         cand_list = load_list("cand_list", cand)
-        d_table = keep.tile([P, G], U32, name="d_table", align_bytes=64)
-        nc.sync.dma_start(d_table[:].bitcast(I32), d_words[0].rearrange("p c r -> p (c r)").bitcast(I32))
         n1_list = load_list("n1_list", n1)
         n2_list = load_list("n2_list", n2)
-
         gs_col = keep.tile([P, PACK], F32, name="gs_col")
-        nc.gpsimd.dma_start(gs_col[:], gs.rearrange("(p t) o -> p (t o)", t=PACK))
-        ident = keep.tile([P, P], F32, name="ident")
-        make_identity(nc, ident[:])
+        nc.sync.dma_start(gs_col[:], gs.rearrange("(p t) o -> p (t o)", t=PACK))
+        x_table = keep.tile([P, T], U32, name="x_table", align_bytes=64)
+        nc.sync.dma_start(x_table[:].bitcast(I32), x_words[0].rearrange("p c r -> p (c r)").bitcast(I32))
+        d_table = keep.tile([P, G], U32, name="d_table", align_bytes=64)
+        nc.sync.dma_start(d_table[:].bitcast(I32), d_words[0].rearrange("p c r -> p (c r)").bitcast(I32))
+
 
         XQ, DA, DB = 0, S, S + H
         picked = keep.tile([P, 2 * H + S], U8, name="picked", align_bytes=64)
@@ -70,21 +72,26 @@ def tile_picked_aqcifill_none_po_kernel(tc, x_words, x_scales, d_words, d_scales
         xc_picked = keep.tile([P, C], U8, name="xc_picked", align_bytes=64)
         nc.vector.tensor_copy(xc_picked[:].rearrange("p (t m) -> p m t", t=PACK), x_scale_table[:].indirect(cand_list[:]))
         place_scale_rows(xc_plane, xc_picked, (nc.sync,))
-        xq_words = keep.tile([P, S], U32, name="xq_words", align_bytes=64)
-        nc.vector.tensor_copy(xq_words[:], x_table[:].indirect(offs_list[:]))
         HALF = H // 2
-        d_picked = {}
+        words = keep.tile([P, S + 2 * H], U32, name="words", align_bytes=64)
+        nc.vector.tensor_copy(words[:, XQ : XQ + S], x_table[:].indirect(offs_list[:]))
         for f in range(2):
-            for part, codes in enumerate((ka_list, kb_list)):
-                words = keep.tile([P, HALF], U32, name="d_picked%d%d" % (f, part), align_bytes=64)
-                nc.vector.tensor_copy(words[:], d_table[:].indirect(codes[:, f * HALF // 16 : (f + 1) * HALF // 16]))
-                d_picked[f, part] = words
+            for start, codes in ((DA, ka_list), (DB, kb_list)):
+                nc.vector.tensor_copy(
+                    words[:, start + f * HALF : start + (f + 1) * HALF],
+                    d_table[:].indirect(codes[:, f * HALF // 16 : (f + 1) * HALF // 16]),
+                )
 
         gs_bank = psum.tile([P, PACK, P], F32, name="gs_bank", tag="turn0")
         for t in range(PACK):
             nc.tensor.transpose(gs_bank[:, t, :], gs_col[:, t : t + 1].to_broadcast([P, P]), ident[:])
         gs_row = keep.tile([P, H], F32, name="gs_row", tag="gs_row", align_bytes=64)
-        nc.scalar.activation(gs_row[:].rearrange("q (p t) -> q p t", t=PACK), gs_bank[:].rearrange("q t p -> q p t"), COPY, scale=SIXTEENTH)
+        nc.scalar.activation(
+            gs_row[:].rearrange("q (u p e) -> q u p e", u=2, e=2),
+            gs_bank[:].rearrange("q (u e) p -> q u p e", u=2),
+            COPY,
+            scale=SIXTEENTH,
+        )
 
         h_banks = {}
         for f in range(2):
@@ -94,9 +101,9 @@ def tile_picked_aqcifill_none_po_kernel(tc, x_words, x_scales, d_words, d_scales
                 for b in range(2):
                     nc.tensor.matmul_mx(
                         out=h_banks[f, b][:],
-                        lhsT=xq_words[:, b * P : (b + 1) * P].bitcast(FP8X4),
+                        lhsT=words[:, XQ + b * P : XQ + (b + 1) * P].bitcast(FP8X4),
                         lhsT_scale=planes[:, XQ + b * P : XQ + (b + 1) * P],
-                        rhs=d_picked[f, part][:].bitcast(FP8X4),
+                        rhs=words[:, start + f * HALF : start + (f + 1) * HALF].bitcast(FP8X4),
                         rhs_scale=planes[:, start + f * HALF : start + (f + 1) * HALF],
                         start=(part == 0),
                         stop=(part == 1),
@@ -105,8 +112,13 @@ def tile_picked_aqcifill_none_po_kernel(tc, x_words, x_scales, d_words, d_scales
         z_rows = [keep.tile([P, H], BF16, name="z_rows%d" % b, align_bytes=64) for b in range(2)]
         for f in range(2):
             for b in range(2):
-                cols = slice(f * HALF, (f + 1) * HALF)
-                nc.vector.tensor_tensor(z_rows[b][:, cols], h_banks[f, b][:], gs_row[:, cols], MULT)
+                rows = slice(f * P // 2, (f + 1) * P // 2)
+                nc.vector.tensor_tensor(
+                    z_rows[b][:].rearrange("q (u p e) -> q u p e", u=2, e=2)[:, :, rows, :],
+                    h_banks[f, b][:].rearrange("q (p u e) -> q u p e", u=2, e=2),
+                    gs_row[:].rearrange("q (u p e) -> q u p e", u=2, e=2)[:, :, rows, :],
+                    MULT,
+                )
 
         z_grouped = keep.tile([P, S * PACK], BF16, name="z_grouped", align_bytes=64)
         z_words = keep.tile([P, S], U32, name="z_words", align_bytes=64)
@@ -115,7 +127,7 @@ def tile_picked_aqcifill_none_po_kernel(tc, x_words, x_scales, d_words, d_scales
             pairs = z_rows[b][:].bitcast(F32)
             turn = psum.tile([P, 2, P], F32, name="turn%d" % b, tag="turn%d" % b)
             for u in range(2):
-                nc.tensor.transpose(turn[:, u, :], pairs[:, u : H // 2 : 2], ident[:])
+                nc.tensor.transpose(turn[:, u, :], pairs[:, u * P : (u + 1) * P], ident[:])
             nc.scalar.copy(
                 z_grouped[:, b * H : (b + 1) * H].bitcast(F32).rearrange("p (r u) -> p r u", u=2),
                 turn[:].rearrange("p u r -> p r u"),
@@ -135,18 +147,21 @@ def tile_picked_aqcifill_none_po_kernel(tc, x_words, x_scales, d_words, d_scales
         y_grouped = keep.tile([P, S, PACK], BF16, name="y_grouped", align_bytes=64)
         s_tiles, pairs_of, larger = [], [], []
         for t in range(PACK):
-            s_bank = psum.tile([P, S], F32, name="s_bank%d" % t, tag="bank%d" % t)
-            nc.tensor.matmul_mx(
-                out=s_bank[:],
-                lhsT=xc_words[:, t * P : (t + 1) * P].bitcast(FP8X4),
-                lhsT_scale=xc_plane[:, t * P : (t + 1) * P],
-                rhs=z_words[:].bitcast(FP8X4),
-                rhs_scale=z_plane[:],
-                start=True,
-                stop=True,
-            )
             s_tile = keep.tile([P, S], F32, name="s_tile%d" % t, align_bytes=64)
-            nc.vector.tensor_scalar(s_tile[:], s_bank[:], SIXTEENTH, None, MULT)
+            pieces = 2 if t == 0 else 1
+            for piece in range(pieces):
+                cols = slice(piece * S // pieces, (piece + 1) * S // pieces)
+                s_bank = psum.tile([P, S // pieces], F32, name="s_bank%d%d" % (t, piece), tag="bank%d" % (t + PACK * piece))
+                nc.tensor.matmul_mx(
+                    out=s_bank[:],
+                    lhsT=xc_words[:, t * P : (t + 1) * P].bitcast(FP8X4),
+                    lhsT_scale=xc_plane[:, t * P : (t + 1) * P],
+                    rhs=z_words[:, cols].bitcast(FP8X4),
+                    rhs_scale=z_plane[:, cols],
+                    start=True,
+                    stop=True,
+                )
+                nc.vector.tensor_scalar(s_tile[:, cols], s_bank[:], SIXTEENTH, None, MULT)
             pair = keep.tile([P, 2 * W], F32, name="pair%d" % t, align_bytes=64)
             nc.scalar.activation(pair[:, 0:W], s_tile[:].indirect(n1_list[:]), COPY)
             nc.scalar.activation(pair[:, W : 2 * W], s_tile[:].indirect(n2_list[:]), COPY)
@@ -170,7 +185,10 @@ def tile_picked_aqcifill_none_po_kernel(tc, x_words, x_scales, d_words, d_scales
                 scales=y_plane[:, b * P : (b + 1) * P],
                 in_=y_grouped[:, b * P : (b + 1) * P, :].rearrange("p j t -> p (j t)"),
             )
-        nc.sync.dma_start(out_1[0].rearrange("p c r -> p (c r)").bitcast(I32), y_words[:].bitcast(I32))
+            nc.sync.dma_start(
+                out_1[0].rearrange("p c r -> p (c r)").bitcast(I32)[:, b * P : (b + 1) * P],
+                y_words[:, b * P : (b + 1) * P].bitcast(I32),
+            )
         for q in range(4):
             queue = nc.scalar if q % 2 == 0 else nc.sync
             queue.dma_start(out_2[0, 4 * q : 4 * q + 4, :].bitcast(I32), y_plane[32 * q : 32 * q + 4, :].bitcast(I32))

@@ -16,12 +16,19 @@ MAX = mybir.AluOpType.max
 
 P = 128
 PACK = 4
+QUADRANT = 32
+BLOCK_PARTITIONS = 8
+LIST_ROWS = 16
 K, T, S, G, H, C, W = 512, 1024, 256, 2048, 512, 512, 128
+HALF = H // 2
+XQ, DA, DB = 0, S, S + H
 SIXTEENTH = 0.0625
 FLOPS = 2 * K * H * S * 2 + 2 * H * C * S
 
 
-def tile_picked_aqcifill_none_po_kernel(tc, x_words, x_scales, d_words, d_scales, gs, offs, ka, kb, cand, n1, n2, out_0, out_1, out_2):
+def tile_picked_aqcifill_none_po_kernel(
+    tc, x_words, x_scales, d_words, d_scales, gs, offs, ka, kb, cand, n1, n2, out_0, out_1, out_2
+):
     nc = tc.nc
     with ExitStack() as ctx:
         keep = ctx.enter_context(tc.tile_pool(name="keep", bufs=1))
@@ -32,54 +39,57 @@ def tile_picked_aqcifill_none_po_kernel(tc, x_words, x_scales, d_words, d_scales
             nc.sync.dma_start(tile[:], source)
             return tile
 
+        def place_scale_rows(plane, source, queues):
+            for a in range(4):
+                queues[a % len(queues)].dma_start(
+                    plane[a:P:QUADRANT, :].bitcast(I32),
+                    source[BLOCK_PARTITIONS * a : P : QUADRANT, :].bitcast(I32),
+                )
+
         d_scale_table = keep.tile([P, G], U8, name="d_scale_table", align_bytes=64)
         x_scale_table = keep.tile([P, T], U8, name="x_scale_table", align_bytes=64)
         nc.gpsimd.memset(x_scale_table[:].bitcast(I32), 0)
         nc.vector.memset(d_scale_table[:].bitcast(I32), 0)
         ident = keep.tile([P, P], F32, name="ident")
         make_identity(nc, ident[:])
-        planes = keep.tile([P, 2 * H + S], U8, name="planes", align_bytes=64)
+        first_plane = keep.tile([P, 2 * H + S], U8, name="planes", align_bytes=64)
         xc_plane = keep.tile([P, C], U8, name="xc_plane", align_bytes=64)
-        nc.vector.memset(planes[:].bitcast(I32), 0)
+        nc.vector.memset(first_plane[:].bitcast(I32), 0)
         nc.vector.memset(xc_plane[:].bitcast(I32), 0)
 
-        def place_scale_rows(plane, source, queues):
-            for a in range(4):
-                queues[a % len(queues)].dma_start(plane[a:P:32, :].bitcast(I32), source[8 * a : P : 32, :].bitcast(I32))
-
         offs_list = load_list("offs_list", offs)
-        nc.scalar.dma_start(x_scale_table[0:P:8, :].bitcast(I32), x_scales[0].bitcast(I32))
+        nc.scalar.dma_start(x_scale_table[0:P:BLOCK_PARTITIONS, :].bitcast(I32), x_scales[0].bitcast(I32))
         ka_list = load_list("ka_list", ka)
-        nc.scalar.dma_start(d_scale_table[0:P:8, :].bitcast(I32), d_scales[0].bitcast(I32))
+        nc.scalar.dma_start(d_scale_table[0:P:BLOCK_PARTITIONS, :].bitcast(I32), d_scales[0].bitcast(I32))
         kb_list = load_list("kb_list", kb)
         cand_list = load_list("cand_list", cand)
         n1_list = load_list("n1_list", n1)
         n2_list = load_list("n2_list", n2)
         gs_col = keep.tile([P, PACK], F32, name="gs_col")
-        nc.sync.dma_start(gs_col[:], gs.rearrange("(p t) o -> p (t o)", t=PACK))
+        nc.gpsimd.dma_start(gs_col[:], gs.rearrange("(p t) o -> p (t o)", t=PACK))
         x_table = keep.tile([P, T], U32, name="x_table", align_bytes=64)
         nc.sync.dma_start(x_table[:].bitcast(I32), x_words[0].rearrange("p c r -> p (c r)").bitcast(I32))
         d_table = keep.tile([P, G], U32, name="d_table", align_bytes=64)
         nc.sync.dma_start(d_table[:].bitcast(I32), d_words[0].rearrange("p c r -> p (c r)").bitcast(I32))
 
-
-        XQ, DA, DB = 0, S, S + H
-        picked = keep.tile([P, 2 * H + S], U8, name="picked", align_bytes=64)
-        nc.vector.tensor_copy(picked[:, XQ : XQ + S], x_scale_table[:].indirect(offs_list[:]))
-        nc.vector.tensor_copy(picked[:, DA : DA + H], d_scale_table[:].indirect(ka_list[:]))
-        nc.vector.tensor_copy(picked[:, DB : DB + H], d_scale_table[:].indirect(kb_list[:]))
-        place_scale_rows(planes, picked, (nc.sync, nc.scalar))
+        first_picked = keep.tile([P, 2 * H + S], U8, name="picked", align_bytes=64)
+        nc.vector.tensor_copy(first_picked[:, XQ : XQ + S], x_scale_table[:].indirect(offs_list[:]))
+        nc.vector.tensor_copy(first_picked[:, DA : DA + H], d_scale_table[:].indirect(ka_list[:]))
+        nc.vector.tensor_copy(first_picked[:, DB : DB + H], d_scale_table[:].indirect(kb_list[:]))
+        place_scale_rows(first_plane, first_picked, (nc.scalar,))
         xc_picked = keep.tile([P, C], U8, name="xc_picked", align_bytes=64)
-        nc.vector.tensor_copy(xc_picked[:].rearrange("p (t m) -> p m t", t=PACK), x_scale_table[:].indirect(cand_list[:]))
+        nc.vector.tensor_copy(
+            xc_picked[:].rearrange("p (t m) -> p m t", t=PACK), x_scale_table[:].indirect(cand_list[:])
+        )
         place_scale_rows(xc_plane, xc_picked, (nc.sync,))
-        HALF = H // 2
-        words = keep.tile([P, S + 2 * H], U32, name="words", align_bytes=64)
-        nc.vector.tensor_copy(words[:, XQ : XQ + S], x_table[:].indirect(offs_list[:]))
+
+        first_words = keep.tile([P, S + 2 * H], U32, name="words", align_bytes=64)
+        nc.vector.tensor_copy(first_words[:, XQ : XQ + S], x_table[:].indirect(offs_list[:]))
         for f in range(2):
-            for start, codes in ((DA, ka_list), (DB, kb_list)):
+            for first, codes in ((DA, ka_list), (DB, kb_list)):
                 nc.vector.tensor_copy(
-                    words[:, start + f * HALF : start + (f + 1) * HALF],
-                    d_table[:].indirect(codes[:, f * HALF // 16 : (f + 1) * HALF // 16]),
+                    first_words[:, first + f * HALF : first + (f + 1) * HALF],
+                    d_table[:].indirect(codes[:, f * HALF // LIST_ROWS : (f + 1) * HALF // LIST_ROWS]),
                 )
 
         gs_bank = psum.tile([P, PACK, P], F32, name="gs_bank", tag="turn0")
@@ -97,26 +107,26 @@ def tile_picked_aqcifill_none_po_kernel(tc, x_words, x_scales, d_words, d_scales
         for f in range(2):
             for b in range(2):
                 h_banks[f, b] = psum.tile([P, HALF], F32, name="h_bank%d%d" % (f, b), tag="bank%d" % (2 * f + b))
-            for part, start in enumerate((DA, DB)):
+            for first in (DA, DB):
                 for b in range(2):
                     nc.tensor.matmul_mx(
                         out=h_banks[f, b][:],
-                        lhsT=words[:, XQ + b * P : XQ + (b + 1) * P].bitcast(FP8X4),
-                        lhsT_scale=planes[:, XQ + b * P : XQ + (b + 1) * P],
-                        rhs=words[:, start + f * HALF : start + (f + 1) * HALF].bitcast(FP8X4),
-                        rhs_scale=planes[:, start + f * HALF : start + (f + 1) * HALF],
-                        start=(part == 0),
-                        stop=(part == 1),
+                        lhsT=first_words[:, XQ + b * P : XQ + (b + 1) * P].bitcast(FP8X4),
+                        lhsT_scale=first_plane[:, XQ + b * P : XQ + (b + 1) * P],
+                        rhs=first_words[:, first + f * HALF : first + (f + 1) * HALF].bitcast(FP8X4),
+                        rhs_scale=first_plane[:, first + f * HALF : first + (f + 1) * HALF],
+                        start=(first == DA),
+                        stop=(first == DB),
                     )
 
         z_rows = [keep.tile([P, H], BF16, name="z_rows%d" % b, align_bytes=64) for b in range(2)]
         for f in range(2):
             for b in range(2):
-                rows = slice(f * P // 2, (f + 1) * P // 2)
+                p_range = slice(f * P // 2, (f + 1) * P // 2)
                 nc.vector.tensor_tensor(
-                    z_rows[b][:].rearrange("q (u p e) -> q u p e", u=2, e=2)[:, :, rows, :],
+                    z_rows[b][:].rearrange("q (u p e) -> q u p e", u=2, e=2)[:, :, p_range, :],
                     h_banks[f, b][:].rearrange("q (p u e) -> q u p e", u=2, e=2),
-                    gs_row[:].rearrange("q (u p e) -> q u p e", u=2, e=2)[:, :, rows, :],
+                    gs_row[:].rearrange("q (u p e) -> q u p e", u=2, e=2)[:, :, p_range, :],
                     MULT,
                 )
 
@@ -124,12 +134,12 @@ def tile_picked_aqcifill_none_po_kernel(tc, x_words, x_scales, d_words, d_scales
         z_words = keep.tile([P, S], U32, name="z_words", align_bytes=64)
         z_plane = keep.tile([P, S], U8, name="z_plane", align_bytes=64)
         for b in range(2):
-            pairs = z_rows[b][:].bitcast(F32)
+            z_pairs = z_rows[b][:].bitcast(F32)
             turn = psum.tile([P, 2, P], F32, name="turn%d" % b, tag="turn%d" % b)
             for u in range(2):
-                nc.tensor.transpose(turn[:, u, :], pairs[:, u * P : (u + 1) * P], ident[:])
+                nc.tensor.transpose(turn[:, u, :], z_pairs[:, u * P : (u + 1) * P], ident[:])
             nc.scalar.copy(
-                z_grouped[:, b * H : (b + 1) * H].bitcast(F32).rearrange("p (r u) -> p r u", u=2),
+                z_grouped[:, b * P * PACK : (b + 1) * P * PACK].bitcast(F32).rearrange("p (r u) -> p r u", u=2),
                 turn[:].rearrange("p u r -> p r u"),
             )
 
@@ -140,18 +150,20 @@ def tile_picked_aqcifill_none_po_kernel(tc, x_words, x_scales, d_words, d_scales
             nc.vector.quantize_mx(
                 out=z_words[:, b * P : (b + 1) * P].bitcast(FP8X4),
                 scales=z_plane[:, b * P : (b + 1) * P],
-                in_=z_grouped[:, b * H : (b + 1) * H],
+                in_=z_grouped[:, b * P * PACK : (b + 1) * P * PACK],
             )
 
         out_rows = out_0.rearrange("(p t) j -> p t j", t=PACK)
         y_grouped = keep.tile([P, S, PACK], BF16, name="y_grouped", align_bytes=64)
-        s_tiles, pairs_of, larger = [], [], []
+        s_tiles, fetched, larger = [], [], []
         for t in range(PACK):
             s_tile = keep.tile([P, S], F32, name="s_tile%d" % t, align_bytes=64)
             pieces = 2 if t == 0 else 1
             for piece in range(pieces):
                 cols = slice(piece * S // pieces, (piece + 1) * S // pieces)
-                s_bank = psum.tile([P, S // pieces], F32, name="s_bank%d%d" % (t, piece), tag="bank%d" % (t + PACK * piece))
+                s_bank = psum.tile(
+                    [P, S // pieces], F32, name="s_bank%d%d" % (t, piece), tag="bank%d" % (t + PACK * piece)
+                )
                 nc.tensor.matmul_mx(
                     out=s_bank[:],
                     lhsT=xc_words[:, t * P : (t + 1) * P].bitcast(FP8X4),
@@ -166,11 +178,12 @@ def tile_picked_aqcifill_none_po_kernel(tc, x_words, x_scales, d_words, d_scales
             nc.scalar.activation(pair[:, 0:W], s_tile[:].indirect(n1_list[:]), COPY)
             nc.scalar.activation(pair[:, W : 2 * W], s_tile[:].indirect(n2_list[:]), COPY)
             s_tiles.append(s_tile)
-            pairs_of.append(pair)
+            fetched.append(pair)
         for t in range(PACK):
             top = keep.tile([P, W], F32, name="larger%d" % t, align_bytes=64)
-            nc.vector.tensor_tensor(top[:], pairs_of[t][:, 0:W], pairs_of[t][:, W : 2 * W], MAX)
+            nc.vector.tensor_tensor(top[:], fetched[t][:, 0:W], fetched[t][:, W : 2 * W], MAX)
             larger.append(top)
+
         for t in range(PACK):
             nc.scalar.activation(s_tiles[t][:].indirect(n1_list[:]), larger[t][:], COPY)
             nc.sync.dma_start(out_rows[:, t, :], s_tiles[t][:])
@@ -191,4 +204,7 @@ def tile_picked_aqcifill_none_po_kernel(tc, x_words, x_scales, d_words, d_scales
             )
         for q in range(4):
             queue = nc.scalar if q % 2 == 0 else nc.sync
-            queue.dma_start(out_2[0, 4 * q : 4 * q + 4, :].bitcast(I32), y_plane[32 * q : 32 * q + 4, :].bitcast(I32))
+            queue.dma_start(
+                out_2[0, 4 * q : 4 * q + 4, :].bitcast(I32),
+                y_plane[QUADRANT * q : QUADRANT * q + 4, :].bitcast(I32),
+            )

from contextlib import ExitStack

import concourse.mybir as mybir
from concourse.masks import make_identity

F32 = mybir.dt.float32
BF16 = mybir.dt.bfloat16
I32 = mybir.dt.int32
U32 = mybir.dt.uint32
U16 = mybir.dt.uint16
U8 = mybir.dt.uint8
FP8X4 = mybir.dt.float8_e4m3fn_x4
COPY = mybir.ActivationFunctionType.Copy
MULT = mybir.AluOpType.mult
MAX = mybir.AluOpType.max

P = 128
PACK = 4
QUADRANT = 32
BLOCK_PARTITIONS = 8
LIST_ROWS = 16
K, T, S, G, H, C, W = 512, 1024, 256, 2048, 512, 512, 128
HALF = H // 2
XQ, DA, DB = 0, S, S + H
SIXTEENTH = 0.0625
FLOPS = 2 * K * H * S * 2 + 2 * H * C * S


def tile_picked_aqcifill_none_po_kernel(
    tc, x_words, x_scales, d_words, d_scales, gs, offs, ka, kb, cand, n1, n2, out_0, out_1, out_2
):
    nc = tc.nc
    with ExitStack() as ctx:
        keep = ctx.enter_context(tc.tile_pool(name="keep", bufs=1))
        psum = ctx.enter_context(tc.psum_pool(name="psum", bufs=1))

        def load_list(name, source):
            tile = keep.tile(list(source.shape), U16, name=name)
            nc.sync.dma_start(tile[:], source)
            return tile

        def place_scale_rows(plane, source, queues):
            for a in range(4):
                queues[a % len(queues)].dma_start(
                    plane[a:P:QUADRANT, :].bitcast(I32),
                    source[BLOCK_PARTITIONS * a : P : QUADRANT, :].bitcast(I32),
                )

        d_scale_table = keep.tile([P, G], U8, name="d_scale_table", align_bytes=64)
        x_scale_table = keep.tile([P, T], U8, name="x_scale_table", align_bytes=64)
        nc.gpsimd.memset(x_scale_table[:].bitcast(I32), 0)
        nc.vector.memset(d_scale_table[:].bitcast(I32), 0)
        ident = keep.tile([P, P], F32, name="ident")
        make_identity(nc, ident[:])
        first_plane = keep.tile([P, 2 * H + S], U8, name="planes", align_bytes=64)
        xc_plane = keep.tile([P, C], U8, name="xc_plane", align_bytes=64)
        nc.vector.memset(first_plane[:].bitcast(I32), 0)
        nc.vector.memset(xc_plane[:].bitcast(I32), 0)

        offs_list = load_list("offs_list", offs)
        nc.scalar.dma_start(x_scale_table[0:P:BLOCK_PARTITIONS, :].bitcast(I32), x_scales[0].bitcast(I32))
        ka_list = load_list("ka_list", ka)
        nc.scalar.dma_start(d_scale_table[0:P:BLOCK_PARTITIONS, :].bitcast(I32), d_scales[0].bitcast(I32))
        kb_list = load_list("kb_list", kb)
        cand_list = load_list("cand_list", cand)
        n1_list = load_list("n1_list", n1)
        n2_list = load_list("n2_list", n2)
        gs_col = keep.tile([P, PACK], F32, name="gs_col")
        nc.gpsimd.dma_start(gs_col[:], gs.rearrange("(p t) o -> p (t o)", t=PACK))
        x_table = keep.tile([P, T], U32, name="x_table", align_bytes=64)
        nc.sync.dma_start(x_table[:].bitcast(I32), x_words[0].rearrange("p c r -> p (c r)").bitcast(I32))
        d_table = keep.tile([P, G], U32, name="d_table", align_bytes=64)
        nc.sync.dma_start(d_table[:].bitcast(I32), d_words[0].rearrange("p c r -> p (c r)").bitcast(I32))

        first_picked = keep.tile([P, 2 * H + S], U8, name="picked", align_bytes=64)
        nc.vector.tensor_copy(first_picked[:, XQ : XQ + S], x_scale_table[:].indirect(offs_list[:]))
        nc.vector.tensor_copy(first_picked[:, DA : DA + H], d_scale_table[:].indirect(ka_list[:]))
        nc.vector.tensor_copy(first_picked[:, DB : DB + H], d_scale_table[:].indirect(kb_list[:]))
        place_scale_rows(first_plane, first_picked, (nc.scalar,))
        xc_picked = keep.tile([P, C], U8, name="xc_picked", align_bytes=64)
        nc.vector.tensor_copy(
            xc_picked[:].rearrange("p (t m) -> p m t", t=PACK), x_scale_table[:].indirect(cand_list[:])
        )
        place_scale_rows(xc_plane, xc_picked, (nc.sync,))

        first_words = keep.tile([P, S + 2 * H], U32, name="words", align_bytes=64)
        nc.vector.tensor_copy(first_words[:, XQ : XQ + S], x_table[:].indirect(offs_list[:]))
        for f in range(2):
            for first, codes in ((DA, ka_list), (DB, kb_list)):
                nc.vector.tensor_copy(
                    first_words[:, first + f * HALF : first + (f + 1) * HALF],
                    d_table[:].indirect(codes[:, f * HALF // LIST_ROWS : (f + 1) * HALF // LIST_ROWS]),
                )

        gs_bank = psum.tile([P, PACK, P], F32, name="gs_bank", tag="turn0")
        for t in range(PACK):
            nc.tensor.transpose(gs_bank[:, t, :], gs_col[:, t : t + 1].to_broadcast([P, P]), ident[:])
        gs_row = keep.tile([P, H], F32, name="gs_row", tag="gs_row", align_bytes=64)
        nc.scalar.activation(
            gs_row[:].rearrange("q (u p e) -> q u p e", u=2, e=2),
            gs_bank[:].rearrange("q (u e) p -> q u p e", u=2),
            COPY,
            scale=SIXTEENTH,
        )

        h_banks = {}
        for f in range(2):
            for b in range(2):
                h_banks[f, b] = psum.tile([P, HALF], F32, name="h_bank%d%d" % (f, b), tag="bank%d" % (2 * f + b))
            for first in (DA, DB):
                for b in range(2):
                    nc.tensor.matmul_mx(
                        out=h_banks[f, b][:],
                        lhsT=first_words[:, XQ + b * P : XQ + (b + 1) * P].bitcast(FP8X4),
                        lhsT_scale=first_plane[:, XQ + b * P : XQ + (b + 1) * P],
                        rhs=first_words[:, first + f * HALF : first + (f + 1) * HALF].bitcast(FP8X4),
                        rhs_scale=first_plane[:, first + f * HALF : first + (f + 1) * HALF],
                        start=(first == DA),
                        stop=(first == DB),
                    )

        z_rows = [keep.tile([P, H], BF16, name="z_rows%d" % b, align_bytes=64) for b in range(2)]
        for f in range(2):
            for b in range(2):
                p_range = slice(f * P // 2, (f + 1) * P // 2)
                nc.vector.tensor_tensor(
                    z_rows[b][:].rearrange("q (u p e) -> q u p e", u=2, e=2)[:, :, p_range, :],
                    h_banks[f, b][:].rearrange("q (p u e) -> q u p e", u=2, e=2),
                    gs_row[:].rearrange("q (u p e) -> q u p e", u=2, e=2)[:, :, p_range, :],
                    MULT,
                )

        z_grouped = keep.tile([P, S * PACK], BF16, name="z_grouped", align_bytes=64)
        z_words = keep.tile([P, S], U32, name="z_words", align_bytes=64)
        z_plane = keep.tile([P, S], U8, name="z_plane", align_bytes=64)
        for b in range(2):
            z_pairs = z_rows[b][:].bitcast(F32)
            turn = psum.tile([P, 2, P], F32, name="turn%d" % b, tag="turn%d" % b)
            for u in range(2):
                nc.tensor.transpose(turn[:, u, :], z_pairs[:, u * P : (u + 1) * P], ident[:])
            nc.scalar.copy(
                z_grouped[:, b * P * PACK : (b + 1) * P * PACK].bitcast(F32).rearrange("p (r u) -> p r u", u=2),
                turn[:].rearrange("p u r -> p r u"),
            )

        xc_words = keep.tile([P, C], U32, name="xc_words", tag="gs_row", align_bytes=64)
        nc.vector.tensor_copy(xc_words[:].rearrange("p (t m) -> p m t", t=PACK), x_table[:].indirect(cand_list[:]))

        for b in range(2):
            nc.vector.quantize_mx(
                out=z_words[:, b * P : (b + 1) * P].bitcast(FP8X4),
                scales=z_plane[:, b * P : (b + 1) * P],
                in_=z_grouped[:, b * P * PACK : (b + 1) * P * PACK],
            )

        out_rows = out_0.rearrange("(p t) j -> p t j", t=PACK)
        y_grouped = keep.tile([P, S, PACK], BF16, name="y_grouped", align_bytes=64)
        s_tiles, fetched, larger = [], [], []
        for t in range(PACK):
            s_tile = keep.tile([P, S], F32, name="s_tile%d" % t, align_bytes=64)
            pieces = 2 if t == 0 else 1
            for piece in range(pieces):
                cols = slice(piece * S // pieces, (piece + 1) * S // pieces)
                s_bank = psum.tile(
                    [P, S // pieces], F32, name="s_bank%d%d" % (t, piece), tag="bank%d" % (t + PACK * piece)
                )
                nc.tensor.matmul_mx(
                    out=s_bank[:],
                    lhsT=xc_words[:, t * P : (t + 1) * P].bitcast(FP8X4),
                    lhsT_scale=xc_plane[:, t * P : (t + 1) * P],
                    rhs=z_words[:, cols].bitcast(FP8X4),
                    rhs_scale=z_plane[:, cols],
                    start=True,
                    stop=True,
                )
                nc.vector.tensor_scalar(s_tile[:, cols], s_bank[:], SIXTEENTH, None, MULT)
            pair = keep.tile([P, 2 * W], F32, name="pair%d" % t, align_bytes=64)
            nc.scalar.activation(pair[:, 0:W], s_tile[:].indirect(n1_list[:]), COPY)
            nc.scalar.activation(pair[:, W : 2 * W], s_tile[:].indirect(n2_list[:]), COPY)
            s_tiles.append(s_tile)
            fetched.append(pair)
        for t in range(PACK):
            top = keep.tile([P, W], F32, name="larger%d" % t, align_bytes=64)
            nc.vector.tensor_tensor(top[:], fetched[t][:, 0:W], fetched[t][:, W : 2 * W], MAX)
            larger.append(top)

        for t in range(PACK):
            nc.scalar.activation(s_tiles[t][:].indirect(n1_list[:]), larger[t][:], COPY)
            nc.sync.dma_start(out_rows[:, t, :], s_tiles[t][:])
            for b in range(2):
                nc.vector.tensor_copy(y_grouped[:, b * P : (b + 1) * P, t], s_tiles[t][:, b * P : (b + 1) * P])

        y_words = keep.tile([P, S], U32, name="y_words", align_bytes=64)
        y_plane = keep.tile([P, S], U8, name="y_plane", align_bytes=64)
        for b in range(2):
            nc.vector.quantize_mx(
                out=y_words[:, b * P : (b + 1) * P].bitcast(FP8X4),
                scales=y_plane[:, b * P : (b + 1) * P],
                in_=y_grouped[:, b * P : (b + 1) * P, :].rearrange("p j t -> p (j t)"),
            )
            nc.sync.dma_start(
                out_1[0].rearrange("p c r -> p (c r)").bitcast(I32)[:, b * P : (b + 1) * P],
                y_words[:, b * P : (b + 1) * P].bitcast(I32),
            )
        for q in range(4):
            queue = nc.scalar if q % 2 == 0 else nc.sync
            queue.dma_start(
                out_2[0, 4 * q : 4 * q + 4, :].bitcast(I32),
                y_plane[QUADRANT * q : QUADRANT * q + 4, :].bitcast(I32),
            )
